import numpy as np
import ml_dtypes


def mxq(x, axis, fmt="e4m3"):
    dtype, down = {"e4m3": (ml_dtypes.float8_e4m3fn, 7), "e5m2": (ml_dtypes.float8_e5m2, 14)}[fmt]
    v = np.moveaxis(np.asarray(x, np.float32).astype(ml_dtypes.bfloat16).astype(np.float64), axis, -1)
    blocks = v.reshape(v.shape[:-1] + (-1, 32))
    amax = np.abs(blocks).max(-1, keepdims=True)
    byte = np.maximum(np.where(amax > 0, np.frexp(amax)[1] - 1 + 127, 0) - down, 1)
    scale = np.exp2(byte - 127.0)
    codes = (blocks / scale).astype(np.float32).astype(dtype).astype(np.float64)
    return np.moveaxis((codes * scale).reshape(v.shape), -1, axis)


WIDE = False


def mx_kscale(k):
    if not WIDE:
        return np.ones(k)
    levels = np.array([10, -10, 5, -5, 0])
    if k % 512:
        return np.exp2(np.random.permutation(np.resize(levels, k // 32))).repeat(32)
    a = np.empty((k // 512, 16))
    for p in range(k // 512):
        a[p, :8] = np.random.permutation(np.resize(levels, 8))
        for g in range(8):
            far = levels[np.abs(levels - a[p, g]) >= 10]
            a[p, g + 8] = far[np.random.randint(len(far))]
    return np.exp2(a.ravel()).repeat(32)


def f64(x):
    return np.asarray(x).astype(np.float64)


def striped(idx):
    return np.tile(idx.reshape(-1, 16).T, (8, 1)).astype(np.uint16)


def unstriped(offs):
    return offs[:16].T.reshape(-1).astype(np.int64)


E2M1 = np.array([0.0, 0.5, 1.0, 1.5, 2.0, 3.0, 4.0, 6.0, -0.0, -0.5, -1.0, -1.5, -2.0, -3.0, -4.0, -6.0])


def pack_weight(w, fmt):
    k, n = w.shape
    w = f64(np.asarray(w, np.float32).astype(ml_dtypes.bfloat16)).reshape(k // 32, 32, n)
    amax = np.abs(w).max(1)
    if fmt == "e4m3":
        byte = np.frexp(amax)[1] - 1 + 127 - 7
    else:
        mant, ex = np.frexp(amax / 6.0)
        byte = np.where(mant > 0.5, ex, ex - 1) + 127
    byte = np.clip(np.where(amax > 0, byte, 1), 1, 254)
    scaled = (w * np.exp2(127.0 - byte)[:, None, :]).reshape(k, n).astype(np.float32)
    by_word = np.ascontiguousarray(scaled.reshape(k // 512, 128, 4, n).transpose(0, 1, 3, 2))
    if fmt == "e4m3":
        words = by_word.astype(ml_dtypes.float8_e4m3fn).view(np.uint8)
    else:
        c = by_word.astype(ml_dtypes.float4_e2m1fn).view(np.uint8) & 0xF
        words = (c[..., 0::2] | (c[..., 1::2] << 4)).reshape(k // 512, 128, 2 * n)
    return np.ascontiguousarray(words), np.ascontiguousarray(byte.astype(np.uint8).reshape(k // 512, 16, n))


def unpack_weight(words, scales, fmt):
    g, _, n = scales.shape
    words = np.ascontiguousarray(words).reshape(g, 128, n, -1)
    if fmt == "e4m3":
        vals = words.view(ml_dtypes.float8_e4m3fn).astype(np.float64)
    else:
        nib = np.empty((g, 128, n, 4), np.uint8)
        nib[..., 0::2] = words & 0xF
        nib[..., 1::2] = words >> 4
        vals = E2M1[nib]
    vals = vals * np.repeat(np.exp2(scales.astype(np.float64) - 127.0), 8, axis=1)[..., None]
    return vals.transpose(0, 1, 3, 2).reshape(g * 512, n)


def gelu(v):
    return 0.5 * v * (1.0 + np.tanh(np.sqrt(2.0 / np.pi) * (v + 0.044715 * v**3)))


K, H, N, T, S, P = 1536, 512, 768, 4096, 1024, 512

def setup_inputs():
    n = np.random.standard_normal
    s = mx_kscale(K)[:, None]
    u = mx_kscale(H)[:, None]
    tab_words, tab_scales = pack_weight(n((K, T)) * s, "e4m3")
    w2_words, w2_scales = pack_weight(0.5 * n((H, H)) / np.sqrt(H) / u, "e2m1")
    perm = np.random.permutation(S)
    return {
        "tab_words": tab_words, "tab_scales": tab_scales,
        "offs": striped(np.random.permutation(T)[:S]),
        "pos1": striped(perm[:P]),
        "pos2": striped(perm[P:]),
        "w1": (0.7 * n((K, H)) / np.sqrt(K) / s).astype(np.float32),
        "boost": (np.random.uniform(1.0, 3.0, H) * u[:, 0]).astype(np.float32),
        "w2_words": w2_words, "w2_scales": w2_scales,
        "dev": (0.15 * n((H, P))).astype(np.float32),
        "skip": (np.random.choice([-1.0, 1.0], H) * np.random.uniform(0.2, 0.5, H)).astype(np.float32),
        "wgs": np.exp(0.3 * n((128, P))).astype(np.float32),
        "gain": (np.random.uniform(2.0, 5.0, H) * u[:, 0]).astype(np.float32),
        "w3": (n((H, N)) / np.sqrt(H) / u).astype(np.float32),
        "rate": np.random.uniform(0.5, 2.0, N).astype(np.float32),
    }

def reference(tab_words, tab_scales, offs, pos1, pos2, w1, boost, w2_words, w2_scales, dev, skip, wgs, gain, w3, rate):
    v = unpack_weight(tab_words, tab_scales, "e4m3")[:, unstriped(offs)]
    w2 = unpack_weight(w2_words, w2_scales, "e2m1")
    x = mxq(f64(w1), 0, "e4m3").T @ v
    f = f64(boost)[:, None] * (x / (1.0 + np.exp(-x)))
    h = x + (w2.T @ mxq(f, 0, "e4m3"))
    top = h.max(axis=1)
    a = np.exp(h[:, unstriped(pos1)] - top[:, None]) + f64(dev)
    page = f64(skip)[:, None] * h
    page[:, unstriped(pos2)] = np.tile(f64(wgs), (H // 128, 1)) * a
    y = mxq(f64(w3), 0, "e4m3").T @ mxq(f64(gain)[:, None] * page, 0, "e4m3")
    return f64(rate)[:, None] * y

@@ -1,0 +1,338 @@
+from contextlib import ExitStack
+
+import concourse.mybir as mybir
+
+K, H, N, T, S, L = 1536, 512, 768, 4096, 1024, 512
+FLOPS = 2 * K * H * S + 2 * H * H * S + 2 * H * N * S
+
+F32 = mybir.dt.float32
+BF16 = mybir.dt.bfloat16
+I32 = mybir.dt.int32
+U32 = mybir.dt.uint32
+U16 = mybir.dt.uint16
+U8 = mybir.dt.uint8
+FP8X4 = mybir.dt.float8_e4m3fn_x4
+FP4X4 = mybir.dt.float4_e2m1fn_x4
+ACT = mybir.ActivationFunctionType
+ALU = mybir.AluOpType
+AX = mybir.AxisListType
+
+P = 128
+PACK = 4
+K_PASS = P * PACK
+PASSES = K // K_PASS
+BANKS = 8
+XCOLS = S // BANKS
+QUARTER = S // 4
+HALF = S // 2
+N_TILES = N // P
+W3_PIECE = 256
+OUT_CHUNKS = (256, 256, 512)
+
+
+def tile_list_streak_forecast_kernel(
+    tc, tab_words, tab_scales, offs, pos1, pos2, w1, boost, w2_words, w2_scales, dev, skip, wgs, gain, w3, rate, out
+):
+    nc = tc.nc
+    with ExitStack() as ctx:
+        lists = ctx.enter_context(tc.tile_pool(name="lists", bufs=1))
+        keep = ctx.enter_context(tc.tile_pool(name="keep", bufs=1))
+        wide = ctx.enter_context(tc.tile_pool(name="wide", bufs=4))
+        half = ctx.enter_context(tc.tile_pool(name="half", bufs=4))
+        psum = ctx.enter_context(tc.psum_pool(name="psum", bufs=1))
+
+        def bank(b, shape):
+            return psum.tile(shape, F32, name="bank%d" % b, tag="bank%d" % b)
+
+        offs_sb = lists.tile([P, S // 16], U16, name="offs_sb")
+        pos1_sb = lists.tile([P, L // 16], U16, name="pos1_sb")
+        pos2_sb = lists.tile([P, L // 16], U16, name="pos2_sb")
+
+        tab_sb = [keep.tile([P, T], U32, name="tab%d" % a, align_bytes=64) for a in range(PASSES)]
+        w1_raw = [wide.tile([P, PACK, H], F32, name="w1_raw%d" % a, tag="wide", align_bytes=64) for a in range(PASSES)]
+
+        def load_tab(a):
+            nc.sync.dma_start(out=tab_sb[a][:].bitcast(I32), in_=tab_words[a].rearrange("p t i -> p (t i)").bitcast(I32))
+
+        def load_w1(a):
+            rows = w1[a * K_PASS : (a + 1) * K_PASS, :]
+            nc.sync.dma_start(out=w1_raw[a][:], in_=rows.rearrange("(p j) c -> p j c", j=PACK))
+
+        load_w1(0)
+        nc.sync.dma_start(offs_sb[:], offs)
+        load_tab(0)
+        load_w1(1)
+        load_w1(2)
+        w2_raw = keep.tile([P, 2 * H], U8, name="w2_raw", align_bytes=64)
+        nc.sync.dma_start(out=w2_raw[:].bitcast(I32), in_=w2_words[0].bitcast(I32))
+        load_tab(1)
+        load_tab(2)
+        boost_sb = keep.tile([P, PACK], F32, name="boost_sb")
+        skip_sb = keep.tile([P, PACK], F32, name="skip_sb")
+        gain_sb = keep.tile([P, PACK], F32, name="gain_sb")
+        for sb, vec in ((boost_sb, boost), (skip_sb, skip), (gain_sb, gain)):
+            nc.sync.dma_start(out=sb[:], in_=vec.rearrange("(p t) -> p t", t=PACK))
+        nc.sync.dma_start(pos1_sb[:], pos1)
+        nc.sync.dma_start(pos2_sb[:], pos2)
+        w3_raw = keep.tile([P, PACK, N], F32, name="w3_raw")
+        nc.sync.dma_start(out=w3_raw[:], in_=w3.rearrange("(p j) n -> p j n", j=PACK))
+        dev_sb = keep.tile([P, PACK, L], F32, name="dev_sb")
+        nc.sync.dma_start(out=dev_sb[:], in_=dev.rearrange("(p t) j -> p t j", t=PACK))
+        wgs_sb = keep.tile([P, PACK, L], F32, name="wgs_sb")
+        for q in range(4):
+            nc.sync.dma_start(out=wgs_sb[32 * q : 32 * (q + 1)], in_=wgs.rearrange("(p t) j -> p t j", t=PACK))
+        rate_sb = keep.tile([P, N_TILES], F32, name="rate_sb")
+        with nc.allow_non_contiguous_dma(reason="one rate value for each output row"):
+            nc.sync.dma_start(out=rate_sb[:], in_=rate.rearrange("(c p) -> p c", p=P))
+
+        tab_planes = keep.tile([P, T], U8, name="tab_planes", align_bytes=64)
+        nc.vector.memset(tab_planes[:].bitcast(I32), 0)
+        w2_plane_raw = keep.tile([P, H], U8, name="w2_plane_raw", align_bytes=64)
+        nc.vector.memset(w2_plane_raw[:].bitcast(I32), 0)
+        for q in range(4):
+            nc.gpsimd.dma_start(
+                out=tab_planes[32 * q : 32 * q + 4 * PASSES, :].bitcast(I32),
+                in_=tab_scales[:, 4 * q : 4 * q + 4, :].bitcast(I32),
+            )
+        for q in range(4):
+            nc.gpsimd.dma_start(
+                out=w2_plane_raw[32 * q : 32 * q + 4, :].bitcast(I32),
+                in_=w2_scales[0, 4 * q : 4 * q + 4, :].bitcast(I32),
+            )
+
+        w1_codes = [keep.tile([P, H], U32, name="w1_codes%d" % a, align_bytes=64) for a in range(PASSES)]
+        w1_plane = [keep.tile([P, H], U8, name="w1_plane%d" % a, align_bytes=64) for a in range(PASSES)]
+
+        def quantize_w1(a):
+            grouped = half.tile([P, PACK, P, PACK], BF16, name="w1_grouped", tag="half", align_bytes=64)
+            nc.scalar.copy(
+                out=grouped[:].rearrange("p t m j -> p m t j"),
+                in_=w1_raw[a][:].rearrange("p j (m t) -> p m t j", t=PACK),
+            )
+            nc.vector.quantize_mx(
+                out=w1_codes[a][:].bitcast(FP8X4),
+                scales=w1_plane[a][:],
+                in_=grouped[:].rearrange("p t m j -> p (t m j)"),
+            )
+
+        v_planes = keep.tile([P, S], U8, name="v_planes", align_bytes=64)
+        v_codes = [keep.tile([P, S], U32, name="v_codes%d" % a, align_bytes=64) for a in range(PASSES)]
+        x_bank = [bank(e, [P, PACK, XCOLS]) for e in range(BANKS)]
+
+        def x_pass(a, e):
+            cols = slice(e * XCOLS, (e + 1) * XCOLS)
+            for t in range(PACK):
+                rows = slice(t * P, (t + 1) * P)
+                nc.tensor.matmul_mx(
+                    out=x_bank[e][:, t, :],
+                    lhsT=w1_codes[a][:, rows].bitcast(FP8X4),
+                    lhsT_scale=w1_plane[a][:, rows],
+                    rhs=v_codes[a][:, cols].bitcast(FP8X4),
+                    rhs_scale=v_planes[4 * a : P, cols],
+                    start=(a == 0 and t == 0),
+                    stop=(a == PASSES - 1 and t == PACK - 1),
+                )
+
+        quantize_w1(0)
+        nc.vector.tensor_copy(out=v_codes[0][:], in_=tab_sb[0][:].indirect(offs_sb[:]))
+        quantize_w1(1)
+        quantize_w1(2)
+        w2_codes = keep.tile([P, 2 * H], U8, name="w2_codes", align_bytes=64)
+        w2_plane = keep.tile([P, H], U8, name="w2_plane", align_bytes=64)
+        nc.vector.tensor_copy(
+            out=w2_codes[:].rearrange("p (t m b) -> p t m b", t=PACK, b=2),
+            in_=w2_raw[:].rearrange("p (m t b) -> p t m b", t=PACK, b=2),
+        )
+        nc.vector.tensor_copy(
+            out=w2_plane[:].rearrange("p (t m) -> p t m", t=PACK),
+            in_=w2_plane_raw[:].rearrange("p (m t) -> p t m", t=PACK),
+        )
+        nc.vector.tensor_copy(out=v_codes[1][:], in_=tab_sb[1][:].indirect(offs_sb[:]))
+        nc.vector.tensor_copy(out=v_planes[:], in_=tab_planes[:].indirect(offs_sb[:]))
+        for a in range(PASSES - 1):
+            for e in range(BANKS):
+                x_pass(a, e)
+
+        last = PASSES - 1
+        silu = [wide.tile([P, HALF, PACK], F32, name="silu%d" % u, tag="wide", align_bytes=64) for u in range(2)]
+        for q in range(4):
+            nc.vector.tensor_copy(
+                out=v_codes[last][:, q * QUARTER : (q + 1) * QUARTER],
+                in_=tab_sb[last][:].indirect(offs_sb[:, q * QUARTER // 16 : (q + 1) * QUARTER // 16]),
+            )
+            for e in (2 * q, 2 * q + 1):
+                x_pass(last, e)
+                c0 = e * XCOLS % HALF
+                nc.scalar.activation(
+                    out=silu[q // 2][:, c0 : c0 + XCOLS, :],
+                    in_=x_bank[e][:].rearrange("p t j -> p j t"),
+                    func=ACT.Silu,
+                )
+        x_sb = [wide.tile([P, PACK, HALF], F32, name="x_sb%d" % u, tag="wide", align_bytes=64) for u in range(2)]
+        for e in range(BANKS):
+            c0 = e * XCOLS % HALF
+            nc.scalar.copy(out=x_sb[e // 4][:, :, c0 : c0 + XCOLS], in_=x_bank[e][:])
+
+        f_bf = [half.tile([P, HALF, PACK], BF16, name="f_bf%d" % u, tag="half", align_bytes=64) for u in range(2)]
+        f_codes = [keep.tile([P, HALF], U32, name="f_codes%d" % u, align_bytes=64) for u in range(2)]
+        f_plane = [keep.tile([P, HALF], U8, name="f_plane%d" % u, align_bytes=64) for u in range(2)]
+
+        def boost_quarter(q):
+            cols = slice(q % 2 * QUARTER, (q % 2 + 1) * QUARTER)
+            nc.vector.tensor_tensor(
+                out=f_bf[q // 2][:, cols, :],
+                in0=silu[q // 2][:, cols, :],
+                in1=boost_sb[:].unsqueeze(1).to_broadcast([P, QUARTER, PACK]),
+                op=ALU.mult,
+            )
+
+        def quantize_quarter(q):
+            cols = slice(q % 2 * QUARTER, (q % 2 + 1) * QUARTER)
+            nc.vector.quantize_mx(
+                out=f_codes[q // 2][:, cols].bitcast(FP8X4),
+                scales=f_plane[q // 2][:, cols],
+                in_=f_bf[q // 2][:, cols, :].rearrange("p j t -> p (j t)"),
+            )
+
+        boost_quarter(0)
+        for q in range(1, 4):
+            boost_quarter(q)
+            quantize_quarter(q - 1)
+        quantize_quarter(3)
+
+        h_sb = [keep.tile([P, S], F32, name="h%d" % t) for t in range(PACK)]
+        neg_top = [keep.tile([P, 1], F32, name="neg_top%d" % t) for t in range(PACK)]
+        y_bank = {}
+        for u in range(2):
+            for t in range(PACK):
+                y_bank[t, u] = bank(PACK * u + t, [P, HALF])
+                nc.tensor.matmul_mx(
+                    out=y_bank[t, u][:],
+                    lhsT=w2_codes[:, 2 * P * t : 2 * P * (t + 1)].bitcast(FP4X4),
+                    lhsT_scale=w2_plane[:, P * t : P * (t + 1)],
+                    rhs=f_codes[u][:].bitcast(FP8X4),
+                    rhs_scale=f_plane[u][:],
+                    start=True,
+                    stop=True,
+                )
+
+        def add_x(t, u):
+            nc.vector.tensor_tensor(
+                out=h_sb[t][:, u * HALF : (u + 1) * HALF], in0=y_bank[t, u][:], in1=x_sb[u][:, t, :], op=ALU.add
+            )
+
+        def row_top(t):
+            nc.vector.tensor_reduce(out=neg_top[t][:], in_=h_sb[t][:], axis=AX.X, op=ALU.max, negate=True)
+
+        for t0 in (0, 2):
+            add_x(t0, 0)
+            add_x(t0 + 1, 0)
+            add_x(t0, 1)
+            add_x(t0 + 1, 1)
+            row_top(t0)
+            row_top(t0 + 1)
+
+        page = [keep.tile([P, S], F32, name="page%d" % t) for t in range(PACK)]
+        look = [keep.tile([P, L], F32, name="look%d" % t) for t in range(PACK)]
+        for t in range(PACK):
+            nc.scalar.activation(out=look[t][:], in_=h_sb[t][:].indirect(pos1_sb[:]), func=ACT.Exp, bias=neg_top[t][:])
+            nc.scalar.activation(out=page[t][:], in_=h_sb[t][:], func=ACT.Copy, scale=skip_sb[:, t : t + 1])
+
+        w3_codes = keep.tile([P, N], U32, name="w3_codes", align_bytes=64)
+        w3_plane = keep.tile([P, N], U8, name="w3_plane", align_bytes=64)
+        w3_bf = keep.tile([P, N, PACK], BF16, name="w3_bf", align_bytes=64)
+        for c0 in range(0, N, W3_PIECE):
+            cols = slice(c0, c0 + W3_PIECE)
+            nc.scalar.copy(
+                out=w3_bf[:, cols, :].rearrange("p (c i) j -> p c j i", i=4),
+                in_=w3_raw[:, :, cols].rearrange("p j (c i) -> p c j i", i=4),
+            )
+
+        def quantize_w3(c0):
+            cols = slice(c0, c0 + W3_PIECE)
+            nc.vector.quantize_mx(
+                out=w3_codes[:, cols].bitcast(FP8X4),
+                scales=w3_plane[:, cols],
+                in_=w3_bf[:, cols, :].rearrange("p n j -> p (n j)"),
+            )
+
+        starts = [sum(OUT_CHUNKS[:c]) for c in range(len(OUT_CHUNKS))]
+        gained = [keep.tile([P, PACK, w], BF16, name="gained%d" % c, align_bytes=64) for c, w in enumerate(OUT_CHUNKS)]
+
+        def add_dev(t):
+            nc.vector.tensor_tensor(out=look[t][:], in0=look[t][:], in1=dev_sb[:, t, :], op=ALU.add)
+
+        add_dev(0)
+        for t in range(PACK):
+            if t + 1 < PACK:
+                add_dev(t + 1)
+            nc.vector.tensor_tensor(
+                out=page[t][:].indirect(pos2_sb[:]), in0=look[t][:], in1=wgs_sb[:, t, :], op=ALU.mult
+            )
+            if t < PACK - 1:
+                quantize_w3(t * W3_PIECE)
+                for c, w in enumerate(OUT_CHUNKS):
+                    nc.scalar.activation(
+                        out=gained[c][:, t, :],
+                        in_=page[t][:, starts[c] : starts[c] + w],
+                        func=ACT.Copy,
+                        scale=gain_sb[:, t : t + 1],
+                    )
+
+        g_codes = [keep.tile([P, w], U32, name="g_codes%d" % c, align_bytes=64) for c, w in enumerate(OUT_CHUNKS)]
+        g_plane = [keep.tile([P, w], U8, name="g_plane%d" % c, align_bytes=64) for c, w in enumerate(OUT_CHUNKS)]
+        g_bf = [half.tile([P, w, PACK], BF16, name="g_bf%d" % c, tag="half", align_bytes=64) for c, w in enumerate(OUT_CHUNKS)]
+        t = PACK - 1
+        for c, w in enumerate(OUT_CHUNKS):
+            nc.vector.tensor_scalar(
+                out=gained[c][:, t, :],
+                in0=page[t][:, starts[c] : starts[c] + w],
+                scalar1=gain_sb[:, t : t + 1],
+                scalar2=None,
+                op0=ALU.mult,
+            )
+
+        def weave(c):
+            nc.vector.tensor_copy(
+                out=g_bf[c][:].rearrange("p (c i) t -> p c t i", i=4),
+                in_=gained[c][:].rearrange("p t (c i) -> p c t i", i=4),
+            )
+
+        def quantize_page(c):
+            nc.vector.quantize_mx(
+                out=g_codes[c][:].bitcast(FP8X4), scales=g_plane[c][:], in_=g_bf[c][:].rearrange("p j t -> p (j t)")
+            )
+
+        weave(0)
+        for c in range(1, len(OUT_CHUNKS)):
+            quantize_page(c - 1)
+            weave(c)
+        quantize_page(len(OUT_CHUNKS) - 1)
+
+        out_rows = out.rearrange("(n p) j -> p n j", p=P)
+        turn = 0
+        for c, w in enumerate(OUT_CHUNKS):
+            per_tile = 3
+            for n0 in range(0, N_TILES, per_tile):
+                staged = wide.tile([P, per_tile, w], F32, name="staged", tag="wide", align_bytes=64)
+                for n in range(n0, n0 + per_tile):
+                    acc = bank(turn % BANKS, [P, w])
+                    turn = turn + 1
+                    nc.tensor.matmul_mx(
+                        out=acc[:],
+                        lhsT=w3_codes[:, n * P : (n + 1) * P].bitcast(FP8X4),
+                        lhsT_scale=w3_plane[:, n * P : (n + 1) * P],
+                        rhs=g_codes[c][:].bitcast(FP8X4),
+                        rhs_scale=g_plane[c][:],
+                        start=True,
+                        stop=True,
+                    )
+                    if c == len(OUT_CHUNKS) - 1 and n % 2 == 1:
+                        nc.vector.tensor_scalar(
+                            out=staged[:, n - n0, :], in0=acc[:], scalar1=rate_sb[:, n : n + 1], scalar2=None, op0=ALU.mult
+                        )
+                    else:
+                        nc.scalar.activation(
+                            out=staged[:, n - n0, :], in_=acc[:], func=ACT.Copy, scale=rate_sb[:, n : n + 1]
+                        )
+                nc.sync.dma_start(out=out_rows[:, n0 : n0 + per_tile, starts[c] : starts[c] + w], in_=staged[:])

@@ -58,19 +58,20 @@ def tile_list_streak_forecast_kernel(
             rows = w1[a * K_PASS : (a + 1) * K_PASS, :]
             nc.sync.dma_start(out=w1_raw[a][:], in_=rows.rearrange("(p j) c -> p j c", j=PACK))
 
-        load_w1(0)
-        nc.sync.dma_start(offs_sb[:], offs)
         load_tab(0)
+        nc.sync.dma_start(offs_sb[:], offs)
+        load_w1(0)
         load_w1(1)
-        load_w1(2)
         w2_raw = keep.tile([P, 2 * H], U8, name="w2_raw", align_bytes=64)
         nc.sync.dma_start(out=w2_raw[:].bitcast(I32), in_=w2_words[0].bitcast(I32))
-        load_tab(1)
-        load_tab(2)
         boost_sb = keep.tile([P, PACK], F32, name="boost_sb")
+        nc.sync.dma_start(out=boost_sb[:], in_=boost.rearrange("(p t) -> p t", t=PACK))
+        load_tab(1)
+        load_w1(2)
+        load_tab(2)
         skip_sb = keep.tile([P, PACK], F32, name="skip_sb")
         gain_sb = keep.tile([P, PACK], F32, name="gain_sb")
-        for sb, vec in ((boost_sb, boost), (skip_sb, skip), (gain_sb, gain)):
+        for sb, vec in ((skip_sb, skip), (gain_sb, gain)):
             nc.sync.dma_start(out=sb[:], in_=vec.rearrange("(p t) -> p t", t=PACK))
         nc.sync.dma_start(pos1_sb[:], pos1)
         nc.sync.dma_start(pos2_sb[:], pos2)
@@ -104,10 +105,11 @@ def tile_list_streak_forecast_kernel(
         w1_plane = [keep.tile([P, H], U8, name="w1_plane%d" % a, align_bytes=64) for a in range(PASSES)]
 
         def quantize_w1(a):
-            grouped = half.tile([P, PACK, P, PACK], BF16, name="w1_grouped", tag="half", align_bytes=64)
+            pool, tag = (keep, "before_w2_plane") if a == 1 else (half, "half")
+            grouped = pool.tile([P, PACK, P, PACK], BF16, name="w1_grouped", tag=tag, align_bytes=64)
             nc.scalar.copy(
-                out=grouped[:].rearrange("p t m j -> p m t j"),
-                in_=w1_raw[a][:].rearrange("p j (m t) -> p m t j", t=PACK),
+                out=grouped[:].rearrange("p t m j -> p m j t"),
+                in_=w1_raw[a][:].rearrange("p j (m t) -> p m j t", t=PACK),
             )
             nc.vector.quantize_mx(
                 out=w1_codes[a][:].bitcast(FP8X4),
@@ -133,12 +135,13 @@ def tile_list_streak_forecast_kernel(
                     stop=(a == PASSES - 1 and t == PACK - 1),
                 )
 
+        nc.vector.tensor_copy(out=v_planes[:], in_=tab_planes[:].indirect(offs_sb[:]))
         quantize_w1(0)
         nc.vector.tensor_copy(out=v_codes[0][:], in_=tab_sb[0][:].indirect(offs_sb[:]))
         quantize_w1(1)
         quantize_w1(2)
         w2_codes = keep.tile([P, 2 * H], U8, name="w2_codes", align_bytes=64)
-        w2_plane = keep.tile([P, H], U8, name="w2_plane", align_bytes=64)
+        w2_plane = keep.tile([P, H], U8, name="w2_plane", tag="before_w2_plane", align_bytes=64)
         nc.vector.tensor_copy(
             out=w2_codes[:].rearrange("p (t m b) -> p t m b", t=PACK, b=2),
             in_=w2_raw[:].rearrange("p (m t b) -> p t m b", t=PACK, b=2),
@@ -147,8 +150,11 @@ def tile_list_streak_forecast_kernel(
             out=w2_plane[:].rearrange("p (t m) -> p t m", t=PACK),
             in_=w2_plane_raw[:].rearrange("p (m t) -> p t m", t=PACK),
         )
-        nc.vector.tensor_copy(out=v_codes[1][:], in_=tab_sb[1][:].indirect(offs_sb[:]))
-        nc.vector.tensor_copy(out=v_planes[:], in_=tab_planes[:].indirect(offs_sb[:]))
+        for u in range(2):
+            nc.vector.tensor_copy(
+                out=v_codes[1][:, u * HALF : (u + 1) * HALF],
+                in_=tab_sb[1][:].indirect(offs_sb[:, u * HALF // 16 : (u + 1) * HALF // 16]),
+            )
         for a in range(PASSES - 1):
             for e in range(BANKS):
                 x_pass(a, e)
@@ -168,7 +174,10 @@ def tile_list_streak_forecast_kernel(
                     in_=x_bank[e][:].rearrange("p t j -> p j t"),
                     func=ACT.Silu,
                 )
-        x_sb = [wide.tile([P, PACK, HALF], F32, name="x_sb%d" % u, tag="wide", align_bytes=64) for u in range(2)]
+        x_sb = [
+            keep.tile([P, PACK, HALF], F32, name="x_sb0", tag="before_w3", align_bytes=64),
+            wide.tile([P, PACK, HALF], F32, name="x_sb1", tag="wide", align_bytes=64),
+        ]
         for e in range(BANKS):
             c0 = e * XCOLS % HALF
             nc.scalar.copy(out=x_sb[e // 4][:, :, c0 : c0 + XCOLS], in_=x_bank[e][:])
@@ -240,7 +249,7 @@ def tile_list_streak_forecast_kernel(
 
         w3_codes = keep.tile([P, N], U32, name="w3_codes", align_bytes=64)
         w3_plane = keep.tile([P, N], U8, name="w3_plane", align_bytes=64)
-        w3_bf = keep.tile([P, N, PACK], BF16, name="w3_bf", align_bytes=64)
+        w3_bf = keep.tile([P, N, PACK], BF16, name="w3_bf", tag="before_w3", align_bytes=64)
         for c0 in range(0, N, W3_PIECE):
             cols = slice(c0, c0 + W3_PIECE)
             nc.scalar.copy(
@@ -282,20 +291,22 @@ def tile_list_streak_forecast_kernel(
         g_codes = [keep.tile([P, w], U32, name="g_codes%d" % c, align_bytes=64) for c, w in enumerate(OUT_CHUNKS)]
         g_plane = [keep.tile([P, w], U8, name="g_plane%d" % c, align_bytes=64) for c, w in enumerate(OUT_CHUNKS)]
         g_bf = [half.tile([P, w, PACK], BF16, name="g_bf%d" % c, tag="half", align_bytes=64) for c, w in enumerate(OUT_CHUNKS)]
-        t = PACK - 1
-        for c, w in enumerate(OUT_CHUNKS):
+
+        def gain_last(c):
+            t = PACK - 1
             nc.vector.tensor_scalar(
                 out=gained[c][:, t, :],
-                in0=page[t][:, starts[c] : starts[c] + w],
+                in0=page[t][:, starts[c] : starts[c] + OUT_CHUNKS[c]],
                 scalar1=gain_sb[:, t : t + 1],
                 scalar2=None,
                 op0=ALU.mult,
             )
 
-        def weave(c):
+        def weave(c, c0):
+            cols = slice(c0, c0 + QUARTER)
             nc.vector.tensor_copy(
-                out=g_bf[c][:].rearrange("p (c i) t -> p c t i", i=4),
-                in_=gained[c][:].rearrange("p t (c i) -> p c t i", i=4),
+                out=g_bf[c][:, cols, :].rearrange("p (c i) t -> p c t i", i=4),
+                in_=gained[c][:, :, cols].rearrange("p t (c i) -> p c t i", i=4),
             )
 
         def quantize_page(c):
@@ -303,16 +314,22 @@ def tile_list_streak_forecast_kernel(
                 out=g_codes[c][:].bitcast(FP8X4), scales=g_plane[c][:], in_=g_bf[c][:].rearrange("p j t -> p (j t)")
             )
 
-        weave(0)
-        for c in range(1, len(OUT_CHUNKS)):
-            quantize_page(c - 1)
-            weave(c)
-        quantize_page(len(OUT_CHUNKS) - 1)
+        gain_last(0)
+        gain_last(1)
+        weave(0, 0)
+        gain_last(2)
+        quantize_page(0)
+        weave(1, 0)
+        weave(2, 0)
+        quantize_page(1)
+        weave(2, QUARTER)
+        quantize_page(2)
 
         out_rows = out.rearrange("(n p) j -> p n j", p=P)
         turn = 0
         for c, w in enumerate(OUT_CHUNKS):
-            per_tile = 3
+            per_tile = N_TILES * QUARTER // w
+            per_store = HALF // w
             for n0 in range(0, N_TILES, per_tile):
                 staged = wide.tile([P, per_tile, w], F32, name="staged", tag="wide", align_bytes=64)
                 for n in range(n0, n0 + per_tile):
@@ -327,7 +344,7 @@ def tile_list_streak_forecast_kernel(
                         start=True,
                         stop=True,
                     )
-                    if c == len(OUT_CHUNKS) - 1 and n % 2 == 1:
+                    if c == len(OUT_CHUNKS) - 1 and n % 2 == 0:
                         nc.vector.tensor_scalar(
                             out=staged[:, n - n0, :], in0=acc[:], scalar1=rate_sb[:, n : n + 1], scalar2=None, op0=ALU.mult
                         )
@@ -335,4 +352,9 @@ def tile_list_streak_forecast_kernel(
                         nc.scalar.activation(
                             out=staged[:, n - n0, :], in_=acc[:], func=ACT.Copy, scale=rate_sb[:, n : n + 1]
                         )
-                nc.sync.dma_start(out=out_rows[:, n0 : n0 + per_tile, starts[c] : starts[c] + w], in_=staged[:])
+                    if (n + 1) % per_store == 0:
+                        first = n + 1 - per_store
+                        nc.sync.dma_start(
+                            out=out_rows[:, first : n + 1, starts[c] : starts[c] + w],
+                            in_=staged[:, first - n0 : n + 1 - n0, :],
+                        )

@@ -27,7 +27,7 @@ QUARTER = S // 4
 HALF = S // 2
 N_TILES = N // P
 W3_PIECE = 256
-OUT_CHUNKS = (256, 256, 512)
+OUT_CHUNKS = (128, 128, 256, 256, 256)
 
 
 def tile_list_streak_forecast_kernel(
@@ -38,7 +38,7 @@ def tile_list_streak_forecast_kernel(
         lists = ctx.enter_context(tc.tile_pool(name="lists", bufs=1))
         keep = ctx.enter_context(tc.tile_pool(name="keep", bufs=1))
         wide = ctx.enter_context(tc.tile_pool(name="wide", bufs=4))
-        half = ctx.enter_context(tc.tile_pool(name="half", bufs=4))
+        half = ctx.enter_context(tc.tile_pool(name="half", bufs=3))
         psum = ctx.enter_context(tc.psum_pool(name="psum", bufs=1))
 
         def bank(b, shape):
@@ -58,15 +58,29 @@ def tile_list_streak_forecast_kernel(
             rows = w1[a * K_PASS : (a + 1) * K_PASS, :]
             nc.sync.dma_start(out=w1_raw[a][:], in_=rows.rearrange("(p j) c -> p j c", j=PACK))
 
+        tab_planes = keep.tile([P, T], U8, name="tab_planes", align_bytes=64)
+        nc.vector.memset(tab_planes[:].bitcast(I32), 0)
+        w2_plane_raw = keep.tile([P, H], U8, name="w2_plane_raw", align_bytes=64)
+        nc.vector.memset(w2_plane_raw[:].bitcast(I32), 0)
         load_tab(0)
+        for q in range(4):
+            nc.sync.dma_start(
+                out=tab_planes[32 * q : 32 * q + 4 * PASSES, :].bitcast(I32),
+                in_=tab_scales[:, 4 * q : 4 * q + 4, :].bitcast(I32),
+            )
         nc.sync.dma_start(offs_sb[:], offs)
         load_w1(0)
         load_w1(1)
+        load_tab(1)
         w2_raw = keep.tile([P, 2 * H], U8, name="w2_raw", align_bytes=64)
         nc.sync.dma_start(out=w2_raw[:].bitcast(I32), in_=w2_words[0].bitcast(I32))
         boost_sb = keep.tile([P, PACK], F32, name="boost_sb")
         nc.sync.dma_start(out=boost_sb[:], in_=boost.rearrange("(p t) -> p t", t=PACK))
-        load_tab(1)
+        for q in range(4):
+            nc.sync.dma_start(
+                out=w2_plane_raw[32 * q : 32 * q + 4, :].bitcast(I32),
+                in_=w2_scales[0, 4 * q : 4 * q + 4, :].bitcast(I32),
+            )
         load_w1(2)
         load_tab(2)
         skip_sb = keep.tile([P, PACK], F32, name="skip_sb")
@@ -86,27 +100,11 @@ def tile_list_streak_forecast_kernel(
         with nc.allow_non_contiguous_dma(reason="one rate value for each output row"):
             nc.sync.dma_start(out=rate_sb[:], in_=rate.rearrange("(c p) -> p c", p=P))
 
-        tab_planes = keep.tile([P, T], U8, name="tab_planes", align_bytes=64)
-        nc.vector.memset(tab_planes[:].bitcast(I32), 0)
-        w2_plane_raw = keep.tile([P, H], U8, name="w2_plane_raw", align_bytes=64)
-        nc.vector.memset(w2_plane_raw[:].bitcast(I32), 0)
-        for q in range(4):
-            nc.gpsimd.dma_start(
-                out=tab_planes[32 * q : 32 * q + 4 * PASSES, :].bitcast(I32),
-                in_=tab_scales[:, 4 * q : 4 * q + 4, :].bitcast(I32),
-            )
-        for q in range(4):
-            nc.gpsimd.dma_start(
-                out=w2_plane_raw[32 * q : 32 * q + 4, :].bitcast(I32),
-                in_=w2_scales[0, 4 * q : 4 * q + 4, :].bitcast(I32),
-            )
-
         w1_codes = [keep.tile([P, H], U32, name="w1_codes%d" % a, align_bytes=64) for a in range(PASSES)]
         w1_plane = [keep.tile([P, H], U8, name="w1_plane%d" % a, align_bytes=64) for a in range(PASSES)]
 
         def quantize_w1(a):
-            pool, tag = (keep, "before_w2_plane") if a == 1 else (half, "half")
-            grouped = pool.tile([P, PACK, P, PACK], BF16, name="w1_grouped", tag=tag, align_bytes=64)
+            grouped = half.tile([P, PACK, P, PACK], BF16, name="w1_grouped", tag="half", align_bytes=64)
             nc.scalar.copy(
                 out=grouped[:].rearrange("p t m j -> p m j t"),
                 in_=w1_raw[a][:].rearrange("p j (m t) -> p m j t", t=PACK),
@@ -141,7 +139,7 @@ def tile_list_streak_forecast_kernel(
         quantize_w1(1)
         quantize_w1(2)
         w2_codes = keep.tile([P, 2 * H], U8, name="w2_codes", align_bytes=64)
-        w2_plane = keep.tile([P, H], U8, name="w2_plane", tag="before_w2_plane", align_bytes=64)
+        w2_plane = keep.tile([P, H], U8, name="w2_plane", align_bytes=64)
         nc.vector.tensor_copy(
             out=w2_codes[:].rearrange("p (t m b) -> p t m b", t=PACK, b=2),
             in_=w2_raw[:].rearrange("p (m t b) -> p t m b", t=PACK, b=2),
@@ -175,8 +173,8 @@ def tile_list_streak_forecast_kernel(
                     func=ACT.Silu,
                 )
         x_sb = [
-            keep.tile([P, PACK, HALF], F32, name="x_sb0", tag="before_w3", align_bytes=64),
-            wide.tile([P, PACK, HALF], F32, name="x_sb1", tag="wide", align_bytes=64),
+            wide.tile([P, PACK, HALF], F32, name="x_sb0", tag="wide", align_bytes=64),
+            keep.tile([P, PACK, HALF], F32, name="x_sb1", tag="before_w3", align_bytes=64),
         ]
         for e in range(BANKS):
             c0 = e * XCOLS % HALF
@@ -210,7 +208,7 @@ def tile_list_streak_forecast_kernel(
         quantize_quarter(3)
 
         h_sb = [keep.tile([P, S], F32, name="h%d" % t) for t in range(PACK)]
-        neg_top = [keep.tile([P, 1], F32, name="neg_top%d" % t) for t in range(PACK)]
+        neg_top = [keep.tile([P, 1], F32, name="neg_top%d" % t, tag="top_page%d" % t) for t in range(PACK)]
         y_bank = {}
         for u in range(2):
             for t in range(PACK):
@@ -241,11 +239,16 @@ def tile_list_streak_forecast_kernel(
             row_top(t0)
             row_top(t0 + 1)
 
-        page = [keep.tile([P, S], F32, name="page%d" % t) for t in range(PACK)]
+        page = [keep.tile([P, S], F32, name="page%d" % t, tag="top_page%d" % (t + 1)) for t in range(PACK)]
         look = [keep.tile([P, L], F32, name="look%d" % t) for t in range(PACK)]
+        def fill_page(t):
+            nc.scalar.activation(out=page[t][:], in_=h_sb[t][:], func=ACT.Copy, scale=skip_sb[:, t : t + 1])
+
         for t in range(PACK):
             nc.scalar.activation(out=look[t][:], in_=h_sb[t][:].indirect(pos1_sb[:]), func=ACT.Exp, bias=neg_top[t][:])
-            nc.scalar.activation(out=page[t][:], in_=h_sb[t][:], func=ACT.Copy, scale=skip_sb[:, t : t + 1])
+            if t > 0:
+                fill_page(t - 1)
+        fill_page(PACK - 1)
 
         w3_codes = keep.tile([P, N], U32, name="w3_codes", align_bytes=64)
         w3_plane = keep.tile([P, N], U8, name="w3_plane", align_bytes=64)
@@ -266,47 +269,40 @@ def tile_list_streak_forecast_kernel(
             )
 
         starts = [sum(OUT_CHUNKS[:c]) for c in range(len(OUT_CHUNKS))]
-        gained = [keep.tile([P, PACK, w], BF16, name="gained%d" % c, align_bytes=64) for c, w in enumerate(OUT_CHUNKS)]
+        gained = keep.tile([P, PACK, S], BF16, name="gained", align_bytes=64)
 
         def add_dev(t):
-            nc.vector.tensor_tensor(out=look[t][:], in0=look[t][:], in1=dev_sb[:, t, :], op=ALU.add)
+            engine = nc.gpsimd if t < 2 else nc.vector
+            engine.tensor_tensor(out=look[t][:], in0=look[t][:], in1=dev_sb[:, t, :], op=ALU.add)
 
         add_dev(0)
+        add_dev(1)
         for t in range(PACK):
-            if t + 1 < PACK:
-                add_dev(t + 1)
             nc.vector.tensor_tensor(
                 out=page[t][:].indirect(pos2_sb[:]), in0=look[t][:], in1=wgs_sb[:, t, :], op=ALU.mult
             )
+            if t + 2 < PACK:
+                add_dev(t + 2)
             if t < PACK - 1:
                 quantize_w3(t * W3_PIECE)
-                for c, w in enumerate(OUT_CHUNKS):
-                    nc.scalar.activation(
-                        out=gained[c][:, t, :],
-                        in_=page[t][:, starts[c] : starts[c] + w],
-                        func=ACT.Copy,
-                        scale=gain_sb[:, t : t + 1],
-                    )
+                nc.scalar.activation(out=gained[:, t, :], in_=page[t][:], func=ACT.Copy, scale=gain_sb[:, t : t + 1])
 
         g_codes = [keep.tile([P, w], U32, name="g_codes%d" % c, align_bytes=64) for c, w in enumerate(OUT_CHUNKS)]
         g_plane = [keep.tile([P, w], U8, name="g_plane%d" % c, align_bytes=64) for c, w in enumerate(OUT_CHUNKS)]
-        g_bf = [half.tile([P, w, PACK], BF16, name="g_bf%d" % c, tag="half", align_bytes=64) for c, w in enumerate(OUT_CHUNKS)]
+        g_bf = [keep.tile([P, w, PACK], BF16, name="g_bf%d" % c, align_bytes=64) for c, w in enumerate(OUT_CHUNKS)]
 
         def gain_last(c):
             t = PACK - 1
+            cols = slice(starts[c], starts[c] + OUT_CHUNKS[c])
             nc.vector.tensor_scalar(
-                out=gained[c][:, t, :],
-                in0=page[t][:, starts[c] : starts[c] + OUT_CHUNKS[c]],
-                scalar1=gain_sb[:, t : t + 1],
-                scalar2=None,
-                op0=ALU.mult,
+                out=gained[:, t, cols], in0=page[t][:, cols], scalar1=gain_sb[:, t : t + 1], scalar2=None, op0=ALU.mult
             )
 
-        def weave(c, c0):
-            cols = slice(c0, c0 + QUARTER)
+        def weave(c):
+            cols = slice(starts[c], starts[c] + OUT_CHUNKS[c])
             nc.vector.tensor_copy(
-                out=g_bf[c][:, cols, :].rearrange("p (c i) t -> p c t i", i=4),
-                in_=gained[c][:, :, cols].rearrange("p t (c i) -> p c t i", i=4),
+                out=g_bf[c][:].rearrange("p (c i) t -> p c t i", i=4),
+                in_=gained[:, :, cols].rearrange("p t (c i) -> p c t i", i=4),
             )
 
         def quantize_page(c):
@@ -314,22 +310,22 @@ def tile_list_streak_forecast_kernel(
                 out=g_codes[c][:].bitcast(FP8X4), scales=g_plane[c][:], in_=g_bf[c][:].rearrange("p j t -> p (j t)")
             )
 
+        chunks = len(OUT_CHUNKS)
         gain_last(0)
         gain_last(1)
-        weave(0, 0)
-        gain_last(2)
-        quantize_page(0)
-        weave(1, 0)
-        weave(2, 0)
-        quantize_page(1)
-        weave(2, QUARTER)
-        quantize_page(2)
+        for c in range(chunks - 2):
+            weave(c)
+            gain_last(c + 2)
+            quantize_page(c)
+        for step in (weave, quantize_page):
+            step(chunks - 2)
+            step(chunks - 1)
 
         out_rows = out.rearrange("(n p) j -> p n j", p=P)
         turn = 0
         for c, w in enumerate(OUT_CHUNKS):
-            per_tile = N_TILES * QUARTER // w
-            per_store = HALF // w
+            per_tile = N_TILES
+            per_store = 2
             for n0 in range(0, N_TILES, per_tile):
                 staged = wide.tile([P, per_tile, w], F32, name="staged", tag="wide", align_bytes=64)
                 for n in range(n0, n0 + per_tile):
@@ -344,7 +340,7 @@ def tile_list_streak_forecast_kernel(
                         start=True,
                         stop=True,
                     )
-                    if c == len(OUT_CHUNKS) - 1 and n % 2 == 0:
+                    if c >= len(OUT_CHUNKS) - 2 and n % 2 == 0:
                         nc.vector.tensor_scalar(
                             out=staged[:, n - n0, :], in0=acc[:], scalar1=rate_sb[:, n : n + 1], scalar2=None, op0=ALU.mult
                         )

@@ -64,24 +64,24 @@ def tile_list_streak_forecast_kernel(
         nc.vector.memset(w2_plane_raw[:].bitcast(I32), 0)
         load_tab(0)
         for q in range(4):
-            nc.sync.dma_start(
+            nc.gpsimd.dma_start(
                 out=tab_planes[32 * q : 32 * q + 4 * PASSES, :].bitcast(I32),
                 in_=tab_scales[:, 4 * q : 4 * q + 4, :].bitcast(I32),
             )
         nc.sync.dma_start(offs_sb[:], offs)
         load_w1(0)
         load_w1(1)
-        load_tab(1)
+        load_w1(2)
         w2_raw = keep.tile([P, 2 * H], U8, name="w2_raw", align_bytes=64)
         nc.sync.dma_start(out=w2_raw[:].bitcast(I32), in_=w2_words[0].bitcast(I32))
-        boost_sb = keep.tile([P, PACK], F32, name="boost_sb")
-        nc.sync.dma_start(out=boost_sb[:], in_=boost.rearrange("(p t) -> p t", t=PACK))
+        load_tab(1)
         for q in range(4):
             nc.sync.dma_start(
                 out=w2_plane_raw[32 * q : 32 * q + 4, :].bitcast(I32),
                 in_=w2_scales[0, 4 * q : 4 * q + 4, :].bitcast(I32),
             )
-        load_w1(2)
+        boost_sb = keep.tile([P, PACK], F32, name="boost_sb")
+        nc.sync.dma_start(out=boost_sb[:], in_=boost.rearrange("(p t) -> p t", t=PACK))
         load_tab(2)
         skip_sb = keep.tile([P, PACK], F32, name="skip_sb")
         gain_sb = keep.tile([P, PACK], F32, name="gain_sb")
@@ -105,7 +105,8 @@ def tile_list_streak_forecast_kernel(
 
         def quantize_w1(a):
             grouped = half.tile([P, PACK, P, PACK], BF16, name="w1_grouped", tag="half", align_bytes=64)
-            nc.scalar.copy(
+            cast = nc.vector.tensor_copy if a == PASSES - 1 else nc.scalar.copy
+            cast(
                 out=grouped[:].rearrange("p t m j -> p m j t"),
                 in_=w1_raw[a][:].rearrange("p j (m t) -> p m j t", t=PACK),
             )
@@ -172,10 +173,7 @@ def tile_list_streak_forecast_kernel(
                     in_=x_bank[e][:].rearrange("p t j -> p j t"),
                     func=ACT.Silu,
                 )
-        x_sb = [
-            wide.tile([P, PACK, HALF], F32, name="x_sb0", tag="wide", align_bytes=64),
-            keep.tile([P, PACK, HALF], F32, name="x_sb1", tag="before_w3", align_bytes=64),
-        ]
+        x_sb = [wide.tile([P, PACK, HALF], F32, name="x_sb%d" % u, tag="wide", align_bytes=64) for u in range(2)]
         for e in range(BANKS):
             c0 = e * XCOLS % HALF
             nc.scalar.copy(out=x_sb[e // 4][:, :, c0 : c0 + XCOLS], in_=x_bank[e][:])
@@ -231,16 +229,25 @@ def tile_list_streak_forecast_kernel(
         def row_top(t):
             nc.vector.tensor_reduce(out=neg_top[t][:], in_=h_sb[t][:], axis=AX.X, op=ALU.max, negate=True)
 
-        for t0 in (0, 2):
-            add_x(t0, 0)
-            add_x(t0 + 1, 0)
-            add_x(t0, 1)
-            add_x(t0 + 1, 1)
-            row_top(t0)
-            row_top(t0 + 1)
+        t = PACK - 1
+        for u in range(2):
+            cols = slice(u * HALF, (u + 1) * HALF)
+            nc.scalar.copy(out=h_sb[t][:, cols], in_=y_bank[t, u][:])
+            nc.gpsimd.tensor_tensor(out=h_sb[t][:, cols], in0=h_sb[t][:, cols], in1=x_sb[u][:, t, :], op=ALU.add)
+        for t in range(PACK - 1):
+            add_x(t, 0)
+        add_x(0, 1)
+        add_x(1, 1)
+        row_top(0)
+        row_top(1)
+        add_x(2, 1)
+        row_top(2)
+        row_top(PACK - 1)
 
-        page = [keep.tile([P, S], F32, name="page%d" % t, tag="top_page%d" % (t + 1)) for t in range(PACK)]
-        look = [keep.tile([P, L], F32, name="look%d" % t) for t in range(PACK)]
+        page = [keep.tile([P, S], F32, name="page%d" % t, tag="top_page%d" % (t + 1)) for t in range(PACK - 1)]
+        look = [keep.tile([P, L], F32, name="look%d" % t, tag="look%d" % t, align_bytes=64) for t in range(PACK)]
+        page.append(keep.tile([P, S], F32, name="page3", tag="look0", align_bytes=64))
+
         def fill_page(t):
             nc.scalar.activation(out=page[t][:], in_=h_sb[t][:], func=ACT.Copy, scale=skip_sb[:, t : t + 1])
 
@@ -252,7 +259,7 @@ def tile_list_streak_forecast_kernel(
 
         w3_codes = keep.tile([P, N], U32, name="w3_codes", align_bytes=64)
         w3_plane = keep.tile([P, N], U8, name="w3_plane", align_bytes=64)
-        w3_bf = keep.tile([P, N, PACK], BF16, name="w3_bf", tag="before_w3", align_bytes=64)
+        w3_bf = keep.tile([P, N, PACK], BF16, name="w3_bf", tag="look1", align_bytes=64)
         for c0 in range(0, N, W3_PIECE):
             cols = slice(c0, c0 + W3_PIECE)
             nc.scalar.copy(
@@ -325,7 +332,7 @@ def tile_list_streak_forecast_kernel(
         turn = 0
         for c, w in enumerate(OUT_CHUNKS):
             per_tile = N_TILES
-            per_store = 2
+            per_store = 3
             for n0 in range(0, N_TILES, per_tile):
                 staged = wide.tile([P, per_tile, w], F32, name="staged", tag="wide", align_bytes=64)
                 for n in range(n0, n0 + per_tile):

@@ -38,7 +38,7 @@ def tile_list_streak_forecast_kernel(
         lists = ctx.enter_context(tc.tile_pool(name="lists", bufs=1))
         keep = ctx.enter_context(tc.tile_pool(name="keep", bufs=1))
         wide = ctx.enter_context(tc.tile_pool(name="wide", bufs=4))
-        half = ctx.enter_context(tc.tile_pool(name="half", bufs=3))
+        half = ctx.enter_context(tc.tile_pool(name="half", bufs=2))
         psum = ctx.enter_context(tc.psum_pool(name="psum", bufs=1))
 
         def bank(b, shape):
@@ -104,7 +104,8 @@ def tile_list_streak_forecast_kernel(
         w1_plane = [keep.tile([P, H], U8, name="w1_plane%d" % a, align_bytes=64) for a in range(PASSES)]
 
         def quantize_w1(a):
-            grouped = half.tile([P, PACK, P, PACK], BF16, name="w1_grouped", tag="half", align_bytes=64)
+            pool, tag = (keep, "before_planes") if a == 0 else (half, "half")
+            grouped = pool.tile([P, PACK, P, PACK], BF16, name="w1_grouped", tag=tag, align_bytes=64)
             cast = nc.vector.tensor_copy if a == PASSES - 1 else nc.scalar.copy
             cast(
                 out=grouped[:].rearrange("p t m j -> p m j t"),
@@ -116,7 +117,6 @@ def tile_list_streak_forecast_kernel(
                 in_=grouped[:].rearrange("p t m j -> p (t m j)"),
             )
 
-        v_planes = keep.tile([P, S], U8, name="v_planes", align_bytes=64)
         v_codes = [keep.tile([P, S], U32, name="v_codes%d" % a, align_bytes=64) for a in range(PASSES)]
         x_bank = [bank(e, [P, PACK, XCOLS]) for e in range(BANKS)]
 
@@ -134,9 +134,10 @@ def tile_list_streak_forecast_kernel(
                     stop=(a == PASSES - 1 and t == PACK - 1),
                 )
 
-        nc.vector.tensor_copy(out=v_planes[:], in_=tab_planes[:].indirect(offs_sb[:]))
         quantize_w1(0)
         nc.vector.tensor_copy(out=v_codes[0][:], in_=tab_sb[0][:].indirect(offs_sb[:]))
+        v_planes = keep.tile([P, S], U8, name="v_planes", tag="before_planes", align_bytes=64)
+        nc.vector.tensor_copy(out=v_planes[:], in_=tab_planes[:].indirect(offs_sb[:]))
         quantize_w1(1)
         quantize_w1(2)
         w2_codes = keep.tile([P, 2 * H], U8, name="w2_codes", align_bytes=64)
@@ -205,7 +206,7 @@ def tile_list_streak_forecast_kernel(
             quantize_quarter(q - 1)
         quantize_quarter(3)
 
-        h_sb = [keep.tile([P, S], F32, name="h%d" % t) for t in range(PACK)]
+        h_sb = [keep.tile([P, S], F32, name="h%d" % t, tag="h%d" % t, align_bytes=64) for t in range(PACK)]
         neg_top = [keep.tile([P, 1], F32, name="neg_top%d" % t, tag="top_page%d" % t) for t in range(PACK)]
         y_bank = {}
         for u in range(2):
@@ -246,7 +247,7 @@ def tile_list_streak_forecast_kernel(
 
         page = [keep.tile([P, S], F32, name="page%d" % t, tag="top_page%d" % (t + 1)) for t in range(PACK - 1)]
         look = [keep.tile([P, L], F32, name="look%d" % t, tag="look%d" % t, align_bytes=64) for t in range(PACK)]
-        page.append(keep.tile([P, S], F32, name="page3", tag="look0", align_bytes=64))
+        page.append(keep.tile([P, S], F32, name="page3", tag="h0", align_bytes=64))
 
         def fill_page(t):
             nc.scalar.activation(out=page[t][:], in_=h_sb[t][:], func=ACT.Copy, scale=skip_sb[:, t : t + 1])
@@ -259,7 +260,7 @@ def tile_list_streak_forecast_kernel(
 
         w3_codes = keep.tile([P, N], U32, name="w3_codes", align_bytes=64)
         w3_plane = keep.tile([P, N], U8, name="w3_plane", align_bytes=64)
-        w3_bf = keep.tile([P, N, PACK], BF16, name="w3_bf", tag="look1", align_bytes=64)
+        w3_bf = keep.tile([P, N, PACK], BF16, name="w3_bf", tag="h1", align_bytes=64)
         for c0 in range(0, N, W3_PIECE):
             cols = slice(c0, c0 + W3_PIECE)
             nc.scalar.copy(
@@ -279,17 +280,13 @@ def tile_list_streak_forecast_kernel(
         gained = keep.tile([P, PACK, S], BF16, name="gained", align_bytes=64)
 
         def add_dev(t):
-            engine = nc.gpsimd if t < 2 else nc.vector
-            engine.tensor_tensor(out=look[t][:], in0=look[t][:], in1=dev_sb[:, t, :], op=ALU.add)
+            a_sb = keep.tile([P, L], F32, name="a_sb", tag="a_sb")
+            nc.gpsimd.tensor_tensor(out=a_sb[:], in0=look[t][:], in1=dev_sb[:, t, :], op=ALU.add)
+            nc.gpsimd.tensor_tensor(out=look[t][:], in0=a_sb[:], in1=wgs_sb[:, t, :], op=ALU.mult)
 
-        add_dev(0)
-        add_dev(1)
         for t in range(PACK):
-            nc.vector.tensor_tensor(
-                out=page[t][:].indirect(pos2_sb[:]), in0=look[t][:], in1=wgs_sb[:, t, :], op=ALU.mult
-            )
-            if t + 2 < PACK:
-                add_dev(t + 2)
+            add_dev(t)
+            nc.vector.tensor_copy(out=page[t][:].indirect(pos2_sb[:]), in_=look[t][:])
             if t < PACK - 1:
                 quantize_w3(t * W3_PIECE)
                 nc.scalar.activation(out=gained[:, t, :], in_=page[t][:], func=ACT.Copy, scale=gain_sb[:, t : t + 1])

from contextlib import ExitStack

import concourse.mybir as mybir

K, H, N, T, S, L = 1536, 512, 768, 4096, 1024, 512
FLOPS = 2 * K * H * S + 2 * H * H * S + 2 * H * N * S

F32 = mybir.dt.float32
BF16 = mybir.dt.bfloat16
I32 = mybir.dt.int32
U32 = mybir.dt.uint32
U16 = mybir.dt.uint16
U8 = mybir.dt.uint8
FP8X4 = mybir.dt.float8_e4m3fn_x4
FP4X4 = mybir.dt.float4_e2m1fn_x4
ACT = mybir.ActivationFunctionType
ALU = mybir.AluOpType
AX = mybir.AxisListType

P = 128
PACK = 4
K_PASS = P * PACK
PASSES = K // K_PASS
BANKS = 8
XCOLS = S // BANKS
QUARTER = S // 4
HALF = S // 2
N_TILES = N // P
W3_PIECE = 256
OUT_CHUNKS = (128, 128, 256, 256, 256)


def tile_list_streak_forecast_kernel(
    tc, tab_words, tab_scales, offs, pos1, pos2, w1, boost, w2_words, w2_scales, dev, skip, wgs, gain, w3, rate, out
):
    nc = tc.nc
    with ExitStack() as ctx:
        lists = ctx.enter_context(tc.tile_pool(name="lists", bufs=1))
        keep = ctx.enter_context(tc.tile_pool(name="keep", bufs=1))
        wide = ctx.enter_context(tc.tile_pool(name="wide", bufs=4))
        half = ctx.enter_context(tc.tile_pool(name="half", bufs=2))
        psum = ctx.enter_context(tc.psum_pool(name="psum", bufs=1))

        def bank(b, shape):
            return psum.tile(shape, F32, name="bank%d" % b, tag="bank%d" % b)

        offs_sb = lists.tile([P, S // 16], U16, name="offs_sb")
        pos1_sb = lists.tile([P, L // 16], U16, name="pos1_sb")
        pos2_sb = lists.tile([P, L // 16], U16, name="pos2_sb")

        tab_sb = [keep.tile([P, T], U32, name="tab%d" % a, align_bytes=64) for a in range(PASSES)]
        w1_raw = [wide.tile([P, PACK, H], F32, name="w1_raw%d" % a, tag="wide", align_bytes=64) for a in range(PASSES)]

        def load_tab(a):
            nc.sync.dma_start(out=tab_sb[a][:].bitcast(I32), in_=tab_words[a].rearrange("p t i -> p (t i)").bitcast(I32))

        def load_w1(a):
            rows = w1[a * K_PASS : (a + 1) * K_PASS, :]
            nc.sync.dma_start(out=w1_raw[a][:], in_=rows.rearrange("(p j) c -> p j c", j=PACK))

        tab_planes = keep.tile([P, T], U8, name="tab_planes", align_bytes=64)
        nc.vector.memset(tab_planes[:].bitcast(I32), 0)
        w2_plane_raw = keep.tile([P, H], U8, name="w2_plane_raw", align_bytes=64)
        nc.vector.memset(w2_plane_raw[:].bitcast(I32), 0)
        load_tab(0)
        for q in range(4):
            nc.gpsimd.dma_start(
                out=tab_planes[32 * q : 32 * q + 4 * PASSES, :].bitcast(I32),
                in_=tab_scales[:, 4 * q : 4 * q + 4, :].bitcast(I32),
            )
        nc.sync.dma_start(offs_sb[:], offs)
        load_w1(0)
        load_w1(1)
        load_w1(2)
        w2_raw = keep.tile([P, 2 * H], U8, name="w2_raw", align_bytes=64)
        nc.sync.dma_start(out=w2_raw[:].bitcast(I32), in_=w2_words[0].bitcast(I32))
        load_tab(1)
        for q in range(4):
            nc.sync.dma_start(
                out=w2_plane_raw[32 * q : 32 * q + 4, :].bitcast(I32),
                in_=w2_scales[0, 4 * q : 4 * q + 4, :].bitcast(I32),
            )
        boost_sb = keep.tile([P, PACK], F32, name="boost_sb")
        nc.sync.dma_start(out=boost_sb[:], in_=boost.rearrange("(p t) -> p t", t=PACK))
        load_tab(2)
        skip_sb = keep.tile([P, PACK], F32, name="skip_sb")
        gain_sb = keep.tile([P, PACK], F32, name="gain_sb")
        for sb, vec in ((skip_sb, skip), (gain_sb, gain)):
            nc.sync.dma_start(out=sb[:], in_=vec.rearrange("(p t) -> p t", t=PACK))
        nc.sync.dma_start(pos1_sb[:], pos1)
        nc.sync.dma_start(pos2_sb[:], pos2)
        w3_raw = keep.tile([P, PACK, N], F32, name="w3_raw")
        nc.sync.dma_start(out=w3_raw[:], in_=w3.rearrange("(p j) n -> p j n", j=PACK))
        dev_sb = keep.tile([P, PACK, L], F32, name="dev_sb")
        nc.sync.dma_start(out=dev_sb[:], in_=dev.rearrange("(p t) j -> p t j", t=PACK))
        wgs_sb = keep.tile([P, PACK, L], F32, name="wgs_sb")
        for q in range(4):
            nc.sync.dma_start(out=wgs_sb[32 * q : 32 * (q + 1)], in_=wgs.rearrange("(p t) j -> p t j", t=PACK))
        rate_sb = keep.tile([P, N_TILES], F32, name="rate_sb")
        with nc.allow_non_contiguous_dma(reason="one rate value for each output row"):
            nc.sync.dma_start(out=rate_sb[:], in_=rate.rearrange("(c p) -> p c", p=P))

        w1_codes = [keep.tile([P, H], U32, name="w1_codes%d" % a, align_bytes=64) for a in range(PASSES)]
        w1_plane = [keep.tile([P, H], U8, name="w1_plane%d" % a, align_bytes=64) for a in range(PASSES)]

        def quantize_w1(a):
            pool, tag = (keep, "before_planes") if a == 0 else (half, "half")
            grouped = pool.tile([P, PACK, P, PACK], BF16, name="w1_grouped", tag=tag, align_bytes=64)
            cast = nc.vector.tensor_copy if a == PASSES - 1 else nc.scalar.copy
            cast(
                out=grouped[:].rearrange("p t m j -> p m j t"),
                in_=w1_raw[a][:].rearrange("p j (m t) -> p m j t", t=PACK),
            )
            nc.vector.quantize_mx(
                out=w1_codes[a][:].bitcast(FP8X4),
                scales=w1_plane[a][:],
                in_=grouped[:].rearrange("p t m j -> p (t m j)"),
            )

        v_codes = [keep.tile([P, S], U32, name="v_codes%d" % a, align_bytes=64) for a in range(PASSES)]
        x_bank = [bank(e, [P, PACK, XCOLS]) for e in range(BANKS)]

        def x_pass(a, e):
            cols = slice(e * XCOLS, (e + 1) * XCOLS)
            for t in range(PACK):
                rows = slice(t * P, (t + 1) * P)
                nc.tensor.matmul_mx(
                    out=x_bank[e][:, t, :],
                    lhsT=w1_codes[a][:, rows].bitcast(FP8X4),
                    lhsT_scale=w1_plane[a][:, rows],
                    rhs=v_codes[a][:, cols].bitcast(FP8X4),
                    rhs_scale=v_planes[4 * a : P, cols],
                    start=(a == 0 and t == 0),
                    stop=(a == PASSES - 1 and t == PACK - 1),
                )

        quantize_w1(0)
        nc.vector.tensor_copy(out=v_codes[0][:], in_=tab_sb[0][:].indirect(offs_sb[:]))
        v_planes = keep.tile([P, S], U8, name="v_planes", tag="before_planes", align_bytes=64)
        nc.vector.tensor_copy(out=v_planes[:], in_=tab_planes[:].indirect(offs_sb[:]))
        quantize_w1(1)
        quantize_w1(2)
        w2_codes = keep.tile([P, 2 * H], U8, name="w2_codes", align_bytes=64)
        w2_plane = keep.tile([P, H], U8, name="w2_plane", align_bytes=64)
        nc.vector.tensor_copy(
            out=w2_codes[:].rearrange("p (t m b) -> p t m b", t=PACK, b=2),
            in_=w2_raw[:].rearrange("p (m t b) -> p t m b", t=PACK, b=2),
        )
        nc.vector.tensor_copy(
            out=w2_plane[:].rearrange("p (t m) -> p t m", t=PACK),
            in_=w2_plane_raw[:].rearrange("p (m t) -> p t m", t=PACK),
        )
        for u in range(2):
            nc.vector.tensor_copy(
                out=v_codes[1][:, u * HALF : (u + 1) * HALF],
                in_=tab_sb[1][:].indirect(offs_sb[:, u * HALF // 16 : (u + 1) * HALF // 16]),
            )
        for a in range(PASSES - 1):
            for e in range(BANKS):
                x_pass(a, e)

        last = PASSES - 1
        silu = [wide.tile([P, HALF, PACK], F32, name="silu%d" % u, tag="wide", align_bytes=64) for u in range(2)]
        for q in range(4):
            nc.vector.tensor_copy(
                out=v_codes[last][:, q * QUARTER : (q + 1) * QUARTER],
                in_=tab_sb[last][:].indirect(offs_sb[:, q * QUARTER // 16 : (q + 1) * QUARTER // 16]),
            )
            for e in (2 * q, 2 * q + 1):
                x_pass(last, e)
                c0 = e * XCOLS % HALF
                nc.scalar.activation(
                    out=silu[q // 2][:, c0 : c0 + XCOLS, :],
                    in_=x_bank[e][:].rearrange("p t j -> p j t"),
                    func=ACT.Silu,
                )
        x_sb = [wide.tile([P, PACK, HALF], F32, name="x_sb%d" % u, tag="wide", align_bytes=64) for u in range(2)]
        for e in range(BANKS):
            c0 = e * XCOLS % HALF
            nc.scalar.copy(out=x_sb[e // 4][:, :, c0 : c0 + XCOLS], in_=x_bank[e][:])

        f_bf = [half.tile([P, HALF, PACK], BF16, name="f_bf%d" % u, tag="half", align_bytes=64) for u in range(2)]
        f_codes = [keep.tile([P, HALF], U32, name="f_codes%d" % u, align_bytes=64) for u in range(2)]
        f_plane = [keep.tile([P, HALF], U8, name="f_plane%d" % u, align_bytes=64) for u in range(2)]

        def boost_quarter(q):
            cols = slice(q % 2 * QUARTER, (q % 2 + 1) * QUARTER)
            nc.vector.tensor_tensor(
                out=f_bf[q // 2][:, cols, :],
                in0=silu[q // 2][:, cols, :],
                in1=boost_sb[:].unsqueeze(1).to_broadcast([P, QUARTER, PACK]),
                op=ALU.mult,
            )

        def quantize_quarter(q):
            cols = slice(q % 2 * QUARTER, (q % 2 + 1) * QUARTER)
            nc.vector.quantize_mx(
                out=f_codes[q // 2][:, cols].bitcast(FP8X4),
                scales=f_plane[q // 2][:, cols],
                in_=f_bf[q // 2][:, cols, :].rearrange("p j t -> p (j t)"),
            )

        boost_quarter(0)
        for q in range(1, 4):
            boost_quarter(q)
            quantize_quarter(q - 1)
        quantize_quarter(3)

        h_sb = [keep.tile([P, S], F32, name="h%d" % t, tag="h%d" % t, align_bytes=64) for t in range(PACK)]
        neg_top = [keep.tile([P, 1], F32, name="neg_top%d" % t, tag="top_page%d" % t) for t in range(PACK)]
        y_bank = {}
        for u in range(2):
            for t in range(PACK):
                y_bank[t, u] = bank(PACK * u + t, [P, HALF])
                nc.tensor.matmul_mx(
                    out=y_bank[t, u][:],
                    lhsT=w2_codes[:, 2 * P * t : 2 * P * (t + 1)].bitcast(FP4X4),
                    lhsT_scale=w2_plane[:, P * t : P * (t + 1)],
                    rhs=f_codes[u][:].bitcast(FP8X4),
                    rhs_scale=f_plane[u][:],
                    start=True,
                    stop=True,
                )

        def add_x(t, u):
            nc.vector.tensor_tensor(
                out=h_sb[t][:, u * HALF : (u + 1) * HALF], in0=y_bank[t, u][:], in1=x_sb[u][:, t, :], op=ALU.add
            )

        def row_top(t):
            nc.vector.tensor_reduce(out=neg_top[t][:], in_=h_sb[t][:], axis=AX.X, op=ALU.max, negate=True)

        t = PACK - 1
        for u in range(2):
            cols = slice(u * HALF, (u + 1) * HALF)
            nc.scalar.copy(out=h_sb[t][:, cols], in_=y_bank[t, u][:])
            nc.gpsimd.tensor_tensor(out=h_sb[t][:, cols], in0=h_sb[t][:, cols], in1=x_sb[u][:, t, :], op=ALU.add)
        for t in range(PACK - 1):
            add_x(t, 0)
        add_x(0, 1)
        add_x(1, 1)
        row_top(0)
        row_top(1)
        add_x(2, 1)
        row_top(2)
        row_top(PACK - 1)

        page = [keep.tile([P, S], F32, name="page%d" % t, tag="top_page%d" % (t + 1)) for t in range(PACK - 1)]
        look = [keep.tile([P, L], F32, name="look%d" % t, tag="look%d" % t, align_bytes=64) for t in range(PACK)]
        page.append(keep.tile([P, S], F32, name="page3", tag="h0", align_bytes=64))

        def fill_page(t):
            nc.scalar.activation(out=page[t][:], in_=h_sb[t][:], func=ACT.Copy, scale=skip_sb[:, t : t + 1])

        for t in range(PACK):
            nc.scalar.activation(out=look[t][:], in_=h_sb[t][:].indirect(pos1_sb[:]), func=ACT.Exp, bias=neg_top[t][:])
            if t > 0:
                fill_page(t - 1)
        fill_page(PACK - 1)

        w3_codes = keep.tile([P, N], U32, name="w3_codes", align_bytes=64)
        w3_plane = keep.tile([P, N], U8, name="w3_plane", align_bytes=64)
        w3_bf = keep.tile([P, N, PACK], BF16, name="w3_bf", tag="h1", align_bytes=64)
        for c0 in range(0, N, W3_PIECE):
            cols = slice(c0, c0 + W3_PIECE)
            nc.scalar.copy(
                out=w3_bf[:, cols, :].rearrange("p (c i) j -> p c j i", i=4),
                in_=w3_raw[:, :, cols].rearrange("p j (c i) -> p c j i", i=4),
            )

        def quantize_w3(c0):
            cols = slice(c0, c0 + W3_PIECE)
            nc.vector.quantize_mx(
                out=w3_codes[:, cols].bitcast(FP8X4),
                scales=w3_plane[:, cols],
                in_=w3_bf[:, cols, :].rearrange("p n j -> p (n j)"),
            )

        starts = [sum(OUT_CHUNKS[:c]) for c in range(len(OUT_CHUNKS))]
        gained = keep.tile([P, PACK, S], BF16, name="gained", align_bytes=64)

        def add_dev(t):
            a_sb = keep.tile([P, L], F32, name="a_sb", tag="a_sb")
            nc.gpsimd.tensor_tensor(out=a_sb[:], in0=look[t][:], in1=dev_sb[:, t, :], op=ALU.add)
            nc.gpsimd.tensor_tensor(out=look[t][:], in0=a_sb[:], in1=wgs_sb[:, t, :], op=ALU.mult)

        for t in range(PACK):
            add_dev(t)
            nc.vector.tensor_copy(out=page[t][:].indirect(pos2_sb[:]), in_=look[t][:])
            if t < PACK - 1:
                quantize_w3(t * W3_PIECE)
                nc.scalar.activation(out=gained[:, t, :], in_=page[t][:], func=ACT.Copy, scale=gain_sb[:, t : t + 1])

        g_codes = [keep.tile([P, w], U32, name="g_codes%d" % c, align_bytes=64) for c, w in enumerate(OUT_CHUNKS)]
        g_plane = [keep.tile([P, w], U8, name="g_plane%d" % c, align_bytes=64) for c, w in enumerate(OUT_CHUNKS)]
        g_bf = [keep.tile([P, w, PACK], BF16, name="g_bf%d" % c, align_bytes=64) for c, w in enumerate(OUT_CHUNKS)]

        def gain_last(c):
            t = PACK - 1
            cols = slice(starts[c], starts[c] + OUT_CHUNKS[c])
            nc.vector.tensor_scalar(
                out=gained[:, t, cols], in0=page[t][:, cols], scalar1=gain_sb[:, t : t + 1], scalar2=None, op0=ALU.mult
            )

        def weave(c):
            cols = slice(starts[c], starts[c] + OUT_CHUNKS[c])
            nc.vector.tensor_copy(
                out=g_bf[c][:].rearrange("p (c i) t -> p c t i", i=4),
                in_=gained[:, :, cols].rearrange("p t (c i) -> p c t i", i=4),
            )

        def quantize_page(c):
            nc.vector.quantize_mx(
                out=g_codes[c][:].bitcast(FP8X4), scales=g_plane[c][:], in_=g_bf[c][:].rearrange("p j t -> p (j t)")
            )

        chunks = len(OUT_CHUNKS)
        gain_last(0)
        gain_last(1)
        for c in range(chunks - 2):
            weave(c)
            gain_last(c + 2)
            quantize_page(c)
        for step in (weave, quantize_page):
            step(chunks - 2)
            step(chunks - 1)

        out_rows = out.rearrange("(n p) j -> p n j", p=P)
        turn = 0
        for c, w in enumerate(OUT_CHUNKS):
            per_tile = N_TILES
            per_store = 3
            for n0 in range(0, N_TILES, per_tile):
                staged = wide.tile([P, per_tile, w], F32, name="staged", tag="wide", align_bytes=64)
                for n in range(n0, n0 + per_tile):
                    acc = bank(turn % BANKS, [P, w])
                    turn = turn + 1
                    nc.tensor.matmul_mx(
                        out=acc[:],
                        lhsT=w3_codes[:, n * P : (n + 1) * P].bitcast(FP8X4),
                        lhsT_scale=w3_plane[:, n * P : (n + 1) * P],
                        rhs=g_codes[c][:].bitcast(FP8X4),
                        rhs_scale=g_plane[c][:],
                        start=True,
                        stop=True,
                    )
                    if c >= len(OUT_CHUNKS) - 2 and n % 2 == 0:
                        nc.vector.tensor_scalar(
                            out=staged[:, n - n0, :], in0=acc[:], scalar1=rate_sb[:, n : n + 1], scalar2=None, op0=ALU.mult
                        )
                    else:
                        nc.scalar.activation(
                            out=staged[:, n - n0, :], in_=acc[:], func=ACT.Copy, scale=rate_sb[:, n : n + 1]
                        )
                    if (n + 1) % per_store == 0:
                        first = n + 1 - per_store
                        nc.sync.dma_start(
                            out=out_rows[:, first : n + 1, starts[c] : starts[c] + w],
                            in_=staged[:, first - n0 : n + 1 - n0, :],
                        )
